import numpy as np
import ml_dtypes


def mxq(x, axis, fmt="e4m3"):
    dtype, down = {"e4m3": (ml_dtypes.float8_e4m3fn, 7), "e5m2": (ml_dtypes.float8_e5m2, 14)}[fmt]
    v = np.moveaxis(np.asarray(x, np.float32).astype(ml_dtypes.bfloat16).astype(np.float64), axis, -1)
    blocks = v.reshape(v.shape[:-1] + (-1, 32))
    amax = np.abs(blocks).max(-1, keepdims=True)
    byte = np.maximum(np.where(amax > 0, np.frexp(amax)[1] - 1 + 127, 0) - down, 1)
    scale = np.exp2(byte - 127.0)
    codes = (blocks / scale).astype(np.float32).astype(dtype).astype(np.float64)
    return np.moveaxis((codes * scale).reshape(v.shape), -1, axis)


WIDE = False


def mx_kscale(k):
    if not WIDE:
        return np.ones(k)
    levels = np.array([10, -10, 5, -5, 0])
    if k % 512:
        return np.exp2(np.random.permutation(np.resize(levels, k // 32))).repeat(32)
    a = np.empty((k // 512, 16))
    for p in range(k // 512):
        a[p, :8] = np.random.permutation(np.resize(levels, 8))
        for g in range(8):
            far = levels[np.abs(levels - a[p, g]) >= 10]
            a[p, g + 8] = far[np.random.randint(len(far))]
    return np.exp2(a.ravel()).repeat(32)


def f64(x):
    return np.asarray(x).astype(np.float64)


def striped(idx):
    return np.tile(np.asarray(idx).reshape(-1, 16).T, (8, 1)).astype(np.uint16)


def unstriped(offs):
    return offs[:16].T.reshape(-1).astype(np.int64)


E2M1 = np.array([0.0, 0.5, 1.0, 1.5, 2.0, 3.0, 4.0, 6.0, -0.0, -0.5, -1.0, -1.5, -2.0, -3.0, -4.0, -6.0])


def pack_weight(w, fmt):
    k, n = w.shape
    w = f64(np.asarray(w, np.float32).astype(ml_dtypes.bfloat16)).reshape(k // 32, 32, n)
    amax = np.abs(w).max(1)
    if fmt == "e4m3":
        byte = np.frexp(amax)[1] - 1 + 127 - 7
    else:
        mant, ex = np.frexp(amax / 6.0)
        byte = np.where(mant > 0.5, ex, ex - 1) + 127
    byte = np.clip(np.where(amax > 0, byte, 1), 1, 254)
    scaled = (w * np.exp2(127.0 - byte)[:, None, :]).reshape(k, n).astype(np.float32)
    by_word = np.ascontiguousarray(scaled.reshape(k // 512, 128, 4, n).transpose(0, 1, 3, 2))
    if fmt == "e4m3":
        words = by_word.astype(ml_dtypes.float8_e4m3fn).view(np.uint8)
    else:
        c = by_word.astype(ml_dtypes.float4_e2m1fn).view(np.uint8) & 0xF
        words = (c[..., 0::2] | (c[..., 1::2] << 4)).reshape(k // 512, 128, 2 * n)
    return np.ascontiguousarray(words), np.ascontiguousarray(byte.astype(np.uint8).reshape(k // 512, 16, n))


def unpack_weight(words, scales, fmt):
    g, _, n = scales.shape
    words = np.ascontiguousarray(words).reshape(g, 128, n, -1)
    if fmt == "e4m3":
        vals = words.view(ml_dtypes.float8_e4m3fn).astype(np.float64)
    else:
        nib = np.empty((g, 128, n, 4), np.uint8)
        nib[..., 0::2] = words & 0xF
        nib[..., 1::2] = words >> 4
        vals = E2M1[nib]
    vals = vals * np.repeat(np.exp2(scales.astype(np.float64) - 127.0), 8, axis=1)[..., None]
    return vals.transpose(0, 1, 3, 2).reshape(g * 512, n)


def bf(x):
    return np.asarray(x, np.float32).astype(ml_dtypes.bfloat16)


def planes(Y):
    r, m = Y.shape
    b = f64(bf(Y)).reshape(r // 32, 32, m)
    amax = np.abs(b).max(1)
    byte = np.clip(np.where(amax > 0, np.frexp(amax)[1] - 1 + 127 - 7, 1), 1, 254)
    codes = (b * np.exp2(127.0 - byte)[:, None, :]).reshape(r, m).astype(np.float32).astype(ml_dtypes.float8_e4m3fn).view(np.uint8)
    words = codes.reshape(r // 512, 128, 4, m).transpose(0, 1, 3, 2)
    return np.ascontiguousarray(words), np.ascontiguousarray(byte.astype(np.uint8).reshape(r // 512, 16, m))


D, T, I, J, U, Z, E, M, C = 512, 2048, 512, 256, 1024, 1024, 512, 1024, 512


def setup_inputs():
    n = np.random.standard_normal
    idx = np.random.permutation(T)[:I]
    idx2 = np.random.permutation(U)[:J]
    idx3 = np.random.permutation(Z)[:J]
    idx4 = np.random.permutation(M)[:J]
    fd = mx_kscale(D)
    fi = mx_kscale(I)
    fc = mx_kscale(C)
    ti = np.ones(T)
    ti[idx] = fi
    keysp = pack_weight(n((D, T)) / fd[:, None], "e2m1")
    return {
        "keys_words": keysp[0],
        "keys_scales": keysp[1],
        "notes": (n((D, U)) * 1.0 / np.sqrt(D) * fd[:, None]).astype(np.float32),
        "given": (np.random.uniform(0.3, 1.7, (I, Z))).astype(np.float32),
        "rowf": (np.random.uniform(0.02, 0.08, (I, 1)) * fi[:, None]).astype(np.float32),
        "vals": (n((E, T)) / ti).astype(np.float32),
        "wm": (n((C, E)) * 1.0 / np.sqrt(C) * fc[:, None]).astype(np.float32),
        "mstore": (n((C, M)) / fc[:, None]).astype(np.float32),
        "offs": striped(idx),
        "offs2": striped(idx2),
        "offs3": striped(idx3),
        "offs4": striped(idx4),
    }


def reference(keys_words, keys_scales, notes, given, rowf, vals, wm, mstore, offs, offs2, offs3, offs4):
    idx = unstriped(offs)
    idx2 = unstriped(offs2)
    idx3 = unstriped(offs3)
    idx4 = unstriped(offs4)
    keysu = unpack_weight(keys_words, keys_scales, "e2m1")
    keysidxg = keysu[:, idx]
    notesidx2q = mxq(f64(notes)[:, idx2], 0, "e4m3")
    g1 = keysidxg.T @ notesidx2q
    g0 = g1 * f64(given)[:, idx3]
    gr1 = g0 * f64(rowf)
    vt1 = f64(vals)[:, idx].T
    vt1q = mxq(vt1, 0, "e4m3")
    gr1q = mxq(gr1, 0, "e4m3")
    o = vt1q.T @ gr1q
    wmq = mxq(f64(wm), 0, "e4m3")
    mstoreq = mxq(f64(mstore), 0, "e4m3")
    me = wmq.T @ mstoreq
    y = o * me[:, idx4]
    words, scales = planes(y)
    return y, words, scales

@@ -1,0 +1,209 @@
+from contextlib import ExitStack
+
+import concourse.mybir as mybir
+from concourse.masks import make_identity
+
+D, T, I, J, U, Z, E, M, C = 512, 2048, 512, 256, 1024, 1024, 512, 1024, 512
+FLOPS = 2 * D * I * J + 2 * I * E * J + 2 * C * E * M
+
+F32 = mybir.dt.float32
+BF16 = mybir.dt.bfloat16
+I32 = mybir.dt.int32
+U32 = mybir.dt.uint32
+U16 = mybir.dt.uint16
+U8 = mybir.dt.uint8
+FP8X4 = mybir.dt.float8_e4m3fn_x4
+FP4X4 = mybir.dt.float4_e2m1fn_x4
+COPY = mybir.ActivationFunctionType.Copy
+MULT = mybir.AluOpType.mult
+
+P = 128
+PACK = 4
+BANK = 512
+HALF_J = J // 2
+
+
+def woven(dst, src):
+    return (
+        dst.rearrange("p (c i) t -> p c t i", i=4),
+        src.rearrange("p t (c i) -> p c t i", i=4),
+    )
+
+
+def tile_attend_tab_timestable_gains_pl_kernel(
+    tc, keys_words, keys_scales, notes, given, rowf, vals, wm, mstore, offs, offs2, offs3, offs4, out_0, out_1, out_2
+):
+    nc = tc.nc
+    with ExitStack() as ctx:
+        lists = ctx.enter_context(tc.tile_pool(name="lists", bufs=1))
+        keep = ctx.enter_context(tc.tile_pool(name="keep", bufs=1))
+        ring = ctx.enter_context(tc.tile_pool(name="ring", bufs=2))
+        acc = ctx.enter_context(tc.psum_pool(name="acc", bufs=4))
+        turn = ctx.enter_context(tc.psum_pool(name="turn", bufs=2))
+        tab = ctx.enter_context(tc.psum_pool(name="tab", bufs=1))
+
+        def quantise(grouped, width, name, pool=keep):
+            codes = pool.tile([P, width], U32, name=name + "_codes", align_bytes=64)
+            scales = pool.tile([P, width], U8, name=name + "_scales", align_bytes=64)
+            nc.vector.quantize_mx(out=codes[:].bitcast(FP8X4), scales=scales[:], in_=grouped)
+            return codes, scales
+
+        key_scale_pool = keep.tile([P, T], U8, align_bytes=64)
+        nc.gpsimd.memset(key_scale_pool[:].bitcast(I32), 0)
+        ident = keep.tile([P, P], F32)
+        make_identity(nc, ident[:])
+
+        key_word_pool = keep.tile([P, T], U16, align_bytes=64)
+        nc.sync.dma_start(key_word_pool[:].bitcast(I32), keys_words[0].bitcast(I32))
+        token_list = lists.tile([P, I // 16], U16)
+        nc.sync.dma_start(token_list[:], offs)
+        wm_raw = keep.tile([P, PACK, E], F32)
+        nc.sync.dma_start(wm_raw[:], wm.rearrange("(p j) e -> p j e", j=PACK))
+        for q in range(4):
+            nc.sync.dma_start(
+                key_scale_pool[32 * q : 32 * q + 4, :].bitcast(I32), keys_scales[0, 4 * q : 4 * q + 4, :].bitcast(I32)
+            )
+        mstore_raw = keep.tile([P, PACK, M], F32)
+        nc.sync.dma_start(mstore_raw[:], mstore.rearrange("(p j) m -> p j m", j=PACK))
+        note_list = lists.tile([P, J // 16], U16)
+        nc.sync.dma_start(note_list[:], offs2)
+        given_list = lists.tile([P, J // 16], U16)
+        nc.sync.dma_start(given_list[:], offs3)
+        memory_list = lists.tile([P, J // 16], U16)
+        nc.sync.dma_start(memory_list[:], offs4)
+        row_factor = keep.tile([P, PACK], F32)
+        nc.sync.dma_start(row_factor[:], rowf.rearrange("(p r) o -> p (r o)", r=PACK))
+        notes_rows = notes.rearrange("(p t) u -> p t u", t=PACK)
+        note_pools = []
+        for a in range(2):
+            pool_tile = keep.tile([P, 2, U], F32, name="note_pool%d" % a)
+            nc.sync.dma_start(pool_tile[:], notes_rows[:, 2 * a : 2 * a + 2, :])
+            note_pools.append(pool_tile)
+        given_rows = given.rearrange("(p r) z -> p r z", r=PACK)
+        given_pools = []
+        for a in range(2):
+            pool_tile = keep.tile([P, 2, Z], F32, name="given_pool%d" % a)
+            nc.sync.dma_start(pool_tile[:], given_rows[:, 2 * a : 2 * a + 2, :])
+            given_pools.append(pool_tile)
+        vals_rows = vals.rearrange("(p t) n -> p t n", t=PACK)
+        value_pools = []
+        for t in range(PACK):
+            pool_tile = keep.tile([P, T], F32, name="value_pool%d" % t)
+            nc.sync.dma_start(pool_tile[:], vals_rows[:, t, :])
+            value_pools.append(pool_tile)
+
+        key_words = keep.tile([P, I], U16, align_bytes=64)
+        nc.vector.tensor_copy(key_words[:], key_word_pool[:].indirect(token_list[:]))
+        key_scales = keep.tile([P, I], U8, align_bytes=64)
+        nc.vector.tensor_copy(
+            key_scales[:].rearrange("p (r s) -> p s r", r=PACK), key_scale_pool[:].indirect(token_list[:])
+        )
+        key_dealt = keep.tile([P, PACK, P], U16, align_bytes=64)
+        nc.vector.tensor_copy(key_dealt[:], key_words[:].rearrange("p (s r) -> p r s", r=PACK))
+
+        wm_grouped = keep.tile([P, E * PACK], BF16, align_bytes=64)
+        nc.vector.tensor_copy(
+            wm_grouped[:].rearrange("p (t s j) -> p s j t", t=PACK, j=PACK),
+            wm_raw[:].rearrange("p j (s t) -> p s j t", t=PACK),
+        )
+        wm_codes, wm_scales = quantise(wm_grouped[:], E, "wm")
+        memories = [keep.tile([P, M], F32, name="memories%d" % t, tag="memories%d" % t) for t in range(PACK)]
+        store_grouped = [keep.tile([P, BANK, PACK], BF16, name="store_grouped%d" % h, align_bytes=64) for h in range(2)]
+        dst, src = woven(store_grouped[0][:], mstore_raw[:, :, 0:BANK])
+        nc.vector.tensor_copy(dst, src)
+        dst, src = woven(store_grouped[1][:], mstore_raw[:, :, BANK:M])
+        nc.scalar.activation(dst, src, COPY)
+        for h in range(2):
+            codes, scales = quantise(store_grouped[h][:].rearrange("p m j -> p (m j)"), BANK, "store%d" % h)
+            for t in range(PACK):
+                bank = acc.tile([P, BANK], F32, name="bank")
+                cols = slice(t * P, (t + 1) * P)
+                nc.tensor.matmul_mx(
+                    out=bank[:], lhsT=wm_codes[:, cols].bitcast(FP8X4), lhsT_scale=wm_scales[:, cols],
+                    rhs=codes[:].bitcast(FP8X4), rhs_scale=scales[:], start=True, stop=True,
+                )
+                nc.scalar.copy(memories[t][:, h * BANK : (h + 1) * BANK], bank[:])
+
+        notes_picked = keep.tile([P, PACK, J], F32)
+        for t in range(PACK):
+            nc.vector.tensor_copy(notes_picked[:, t, :], note_pools[t // 2][:, t % 2, :].indirect(note_list[:]))
+        notes_grouped = keep.tile([P, J, PACK], BF16, align_bytes=64)
+        dst, src = woven(notes_grouped[:], notes_picked[:])
+        nc.vector.tensor_copy(dst, src)
+        note_codes, note_scales = quantise(notes_grouped[:].rearrange("p j t -> p (j t)"), J, "notes")
+        products = [tab.tile([P, 2, J], F32, name="products%d" % a) for a in range(2)]
+        for r in range(PACK):
+            nc.tensor.matmul_mx(
+                out=products[r // 2][:, r % 2, :], lhsT=key_dealt[:, r, :].bitcast(FP4X4),
+                lhsT_scale=key_scales[:, r * P : (r + 1) * P],
+                rhs=note_codes[:].bitcast(FP8X4), rhs_scale=note_scales[:], start=True, stop=True,
+            )
+
+        memories_picked = []
+        for t in range(PACK):
+            looked_up = keep.tile([P, J], F32, name="memories_picked%d" % t, tag="swap%d" % (t + 1), align_bytes=64)
+            nc.scalar.activation(looked_up[:], memories[t][:].indirect(memory_list[:]), COPY)
+            memories_picked.append(looked_up)
+
+        given_picked = keep.tile([P, PACK, J], F32)
+        table = keep.tile([P, PACK, J], F32)
+        for a in range(2):
+            for r in (2 * a, 2 * a + 1):
+                nc.vector.tensor_copy(given_picked[:, r, :], given_pools[a][:, r % 2, :].indirect(given_list[:]))
+            for r in (2 * a, 2 * a + 1):
+                nc.vector.scalar_tensor_tensor(
+                    table[:, r, :], products[a][:, r % 2, :], row_factor[:, r : r + 1], given_picked[:, r, :], MULT, MULT
+                )
+        table_grouped = keep.tile([P, J, PACK], BF16, align_bytes=64)
+        dst, src = woven(table_grouped[:], table[:])
+        nc.vector.tensor_copy(dst, src)
+        table_codes, table_scales = quantise(table_grouped[:].rearrange("p j r -> p (j r)"), J, "table")
+
+        result = keep.tile([P, PACK, J], F32)
+        result_grouped = [keep.tile([P, HALF_J, PACK], BF16, name="result_grouped%d" % h, align_bytes=64) for h in range(2)]
+        for t in range(PACK):
+            picked = keep.tile([P, I], BF16, name="picked%d" % t, tag="memories%d" % (PACK - 1))
+            nc.scalar.activation(picked[:], value_pools[t][:].indirect(token_list[:]), COPY)
+            pairs = picked[:].bitcast(F32)
+            turned = turn.tile([P, 2, P], F32)
+            for u in range(2):
+                nc.tensor.transpose(turned[:, u, :], pairs[:, u : I // 2 : 2], ident[:])
+            values_grouped = keep.tile([P, P * PACK], BF16, name="values_grouped%d" % t, tag="swap%d" % t, align_bytes=64)
+            copy_out = nc.scalar.copy if t == PACK - 1 else nc.vector.tensor_copy
+            copy_out(
+                values_grouped[:].bitcast(F32).rearrange("p (e u) -> p e u", u=2), turned[:].rearrange("p u e -> p e u")
+            )
+            value_codes, value_scales = quantise(values_grouped[:], P, "values", ring)
+            sums = []
+            for h in range(2):
+                cols = slice(h * HALF_J, (h + 1) * HALF_J)
+                bank = acc.tile([P, BANK], F32, name="bank")
+                nc.tensor.matmul_mx(
+                    out=bank[:, 0:HALF_J], lhsT=value_codes[:].bitcast(FP8X4), lhsT_scale=value_scales[:],
+                    rhs=table_codes[:, cols].bitcast(FP8X4), rhs_scale=table_scales[:, cols], start=True, stop=True,
+                )
+                sums.append(bank)
+            for h in range(2):
+                cols = slice(h * HALF_J, (h + 1) * HALF_J)
+                nc.vector.tensor_tensor(result[:, t, cols], sums[h][:, 0:HALF_J], memories_picked[t][:, cols], MULT)
+            for h in range(2):
+                cols = slice(h * HALF_J, (h + 1) * HALF_J)
+                nc.vector.tensor_copy(result_grouped[h][:, :, t], result[:, t, cols])
+
+        out_rows = out_0.rearrange("(p t) j -> p t j", t=PACK)
+        nc.sync.dma_start(out_rows[:, 0 : PACK - 1, :], result[:, 0 : PACK - 1, :])
+        nc.scalar.dma_start(out_rows[:, PACK - 1, :], result[:, PACK - 1, :])
+        result_codes = keep.tile([P, J], U32, align_bytes=64)
+        result_scales = keep.tile([P, J], U8, align_bytes=64)
+        for h in range(2):
+            cols = slice(h * HALF_J, (h + 1) * HALF_J)
+            nc.vector.quantize_mx(
+                out=result_codes[:, cols].bitcast(FP8X4), scales=result_scales[:, cols],
+                in_=result_grouped[h][:].rearrange("p j t -> p (j t)"),
+            )
+        nc.sync.dma_start(out_1[0].rearrange("p c r -> p (c r)").bitcast(I32), result_codes[:].bitcast(I32))
+        for q in range(4):
+            queue = nc.sync if q < 2 else nc.scalar
+            queue.dma_start(
+                out_2[0, 4 * q : 4 * q + 4, :].bitcast(I32), result_scales[32 * q : 32 * q + 4, :].bitcast(I32)
+            )

@@ -37,7 +37,6 @@ def tile_attend_tab_timestable_gains_pl_kernel(
     with ExitStack() as ctx:
         lists = ctx.enter_context(tc.tile_pool(name="lists", bufs=1))
         keep = ctx.enter_context(tc.tile_pool(name="keep", bufs=1))
-        ring = ctx.enter_context(tc.tile_pool(name="ring", bufs=2))
         acc = ctx.enter_context(tc.psum_pool(name="acc", bufs=4))
         turn = ctx.enter_context(tc.psum_pool(name="turn", bufs=2))
         tab = ctx.enter_context(tc.psum_pool(name="tab", bufs=1))
@@ -48,71 +47,80 @@ def tile_attend_tab_timestable_gains_pl_kernel(
             nc.vector.quantize_mx(out=codes[:].bitcast(FP8X4), scales=scales[:], in_=grouped)
             return codes, scales
 
+        store_rows = mstore.rearrange("(p j) m -> p j m", j=PACK)
+        store_raw = [keep.tile([P, 2, M], F32, name="store_raw%d" % a) for a in range(2)]
+        nc.scalar.dma_start(store_raw[0][:], store_rows[:, 0:2, :])
+
         key_scale_pool = keep.tile([P, T], U8, align_bytes=64)
-        nc.gpsimd.memset(key_scale_pool[:].bitcast(I32), 0)
+        nc.vector.memset(key_scale_pool[:].bitcast(I32), 0)
+        nc.scalar.dma_start(key_scale_pool[0:P:8, :].bitcast(I32), keys_scales[0].bitcast(I32))
+        key_scales = keep.tile([P, I], U8, align_bytes=64)
+        nc.gpsimd.memset(key_scales[:].bitcast(I32), 0)
+        row_factor = keep.tile([P, PACK], F32)
+        nc.scalar.dma_start(row_factor[:], rowf.rearrange("(p r) o -> p (r o)", r=PACK))
         ident = keep.tile([P, P], F32)
         make_identity(nc, ident[:])
 
-        key_word_pool = keep.tile([P, T], U16, align_bytes=64)
-        nc.sync.dma_start(key_word_pool[:].bitcast(I32), keys_words[0].bitcast(I32))
         token_list = lists.tile([P, I // 16], U16)
         nc.sync.dma_start(token_list[:], offs)
-        wm_raw = keep.tile([P, PACK, E], F32)
-        nc.sync.dma_start(wm_raw[:], wm.rearrange("(p j) e -> p j e", j=PACK))
-        for q in range(4):
-            nc.sync.dma_start(
-                key_scale_pool[32 * q : 32 * q + 4, :].bitcast(I32), keys_scales[0, 4 * q : 4 * q + 4, :].bitcast(I32)
-            )
-        mstore_raw = keep.tile([P, PACK, M], F32)
-        nc.sync.dma_start(mstore_raw[:], mstore.rearrange("(p j) m -> p j m", j=PACK))
         note_list = lists.tile([P, J // 16], U16)
         nc.sync.dma_start(note_list[:], offs2)
         given_list = lists.tile([P, J // 16], U16)
         nc.sync.dma_start(given_list[:], offs3)
         memory_list = lists.tile([P, J // 16], U16)
         nc.sync.dma_start(memory_list[:], offs4)
-        row_factor = keep.tile([P, PACK], F32)
-        nc.sync.dma_start(row_factor[:], rowf.rearrange("(p r) o -> p (r o)", r=PACK))
-        notes_rows = notes.rearrange("(p t) u -> p t u", t=PACK)
-        note_pools = []
-        for a in range(2):
-            pool_tile = keep.tile([P, 2, U], F32, name="note_pool%d" % a)
-            nc.sync.dma_start(pool_tile[:], notes_rows[:, 2 * a : 2 * a + 2, :])
-            note_pools.append(pool_tile)
+        wm_raw = keep.tile([P, PACK, E], F32)
+        nc.sync.dma_start(wm_raw[:], wm.rearrange("(p j) e -> p j e", j=PACK))
+        nc.sync.dma_start(store_raw[1][:], store_rows[:, 2:4, :])
+        key_word_pool = keep.tile([P, T], U16, align_bytes=64)
+        nc.sync.dma_start(key_word_pool[:].bitcast(I32), keys_words[0].bitcast(I32))
+        note_pool = keep.tile([P, PACK, U], F32)
+        nc.sync.dma_start(note_pool[:], notes.rearrange("(p t) u -> p t u", t=PACK))
         given_rows = given.rearrange("(p r) z -> p r z", r=PACK)
         given_pools = []
         for a in range(2):
-            pool_tile = keep.tile([P, 2, Z], F32, name="given_pool%d" % a)
+            pool_tile = keep.tile([P, 2, Z], F32, name="given_pool%d" % a, tag="given_pool%d" % a)
             nc.sync.dma_start(pool_tile[:], given_rows[:, 2 * a : 2 * a + 2, :])
             given_pools.append(pool_tile)
         vals_rows = vals.rearrange("(p t) n -> p t n", t=PACK)
         value_pools = []
         for t in range(PACK):
-            pool_tile = keep.tile([P, T], F32, name="value_pool%d" % t)
+            pool_tile = keep.tile([P, T], F32, name="value_pool%d" % t, tag="value_pool%d" % t, align_bytes=64)
             nc.sync.dma_start(pool_tile[:], vals_rows[:, t, :])
             value_pools.append(pool_tile)
 
-        key_words = keep.tile([P, I], U16, align_bytes=64)
-        nc.vector.tensor_copy(key_words[:], key_word_pool[:].indirect(token_list[:]))
-        key_scales = keep.tile([P, I], U8, align_bytes=64)
-        nc.vector.tensor_copy(
-            key_scales[:].rearrange("p (r s) -> p s r", r=PACK), key_scale_pool[:].indirect(token_list[:])
-        )
-        key_dealt = keep.tile([P, PACK, P], U16, align_bytes=64)
-        nc.vector.tensor_copy(key_dealt[:], key_words[:].rearrange("p (s r) -> p r s", r=PACK))
+        store_grouped = [
+            keep.tile([P, BANK, PACK], BF16, name="store_grouped%d" % h, tag="store_grouped%d" % h, align_bytes=64)
+            for h in range(2)
+        ]
 
+        def round_store(a, h):
+            dst, src = woven(store_grouped[h][:, :, 2 * a : 2 * a + 2], store_raw[a][:, :, h * BANK : (h + 1) * BANK])
+            if a == 0:
+                nc.scalar.activation(dst, src, COPY)
+            else:
+                nc.vector.tensor_copy(dst, src)
+
+        round_store(0, 0)
+        round_store(0, 1)
         wm_grouped = keep.tile([P, E * PACK], BF16, align_bytes=64)
         nc.vector.tensor_copy(
             wm_grouped[:].rearrange("p (t s j) -> p s j t", t=PACK, j=PACK),
             wm_raw[:].rearrange("p j (s t) -> p s j t", t=PACK),
         )
         wm_codes, wm_scales = quantise(wm_grouped[:], E, "wm")
+        scales_picked = keep.tile([P, I], U8, align_bytes=64)
+        nc.vector.tensor_copy(
+            scales_picked[:].rearrange("p (r s) -> p s r", r=PACK), key_scale_pool[:].indirect(token_list[:])
+        )
+        for q in range(4):
+            nc.scalar.dma_start(
+                key_scales[32 * q : 32 * q + 4, :].bitcast(I32), scales_picked[32 * q : 32 * q + 32 : 8, :].bitcast(I32)
+            )
+
         memories = [keep.tile([P, M], F32, name="memories%d" % t, tag="memories%d" % t) for t in range(PACK)]
-        store_grouped = [keep.tile([P, BANK, PACK], BF16, name="store_grouped%d" % h, align_bytes=64) for h in range(2)]
-        dst, src = woven(store_grouped[0][:], mstore_raw[:, :, 0:BANK])
-        nc.vector.tensor_copy(dst, src)
-        dst, src = woven(store_grouped[1][:], mstore_raw[:, :, BANK:M])
-        nc.scalar.activation(dst, src, COPY)
+        round_store(1, 0)
+        round_store(1, 1)
         for h in range(2):
             codes, scales = quantise(store_grouped[h][:].rearrange("p m j -> p (m j)"), BANK, "store%d" % h)
             for t in range(PACK):
@@ -122,11 +130,16 @@ def tile_attend_tab_timestable_gains_pl_kernel(
                     out=bank[:], lhsT=wm_codes[:, cols].bitcast(FP8X4), lhsT_scale=wm_scales[:, cols],
                     rhs=codes[:].bitcast(FP8X4), rhs_scale=scales[:], start=True, stop=True,
                 )
-                nc.scalar.copy(memories[t][:, h * BANK : (h + 1) * BANK], bank[:])
+                nc.scalar.activation(memories[t][:, h * BANK : (h + 1) * BANK], bank[:], COPY)
+
+        key_words = keep.tile([P, I], U16, tag="store_grouped0", align_bytes=64)
+        nc.vector.tensor_copy(key_words[:], key_word_pool[:].indirect(token_list[:]))
+        key_dealt = keep.tile([P, PACK, P], U16, align_bytes=64)
+        nc.vector.tensor_copy(key_dealt[:], key_words[:].rearrange("p (s r) -> p r s", r=PACK))
 
         notes_picked = keep.tile([P, PACK, J], F32)
         for t in range(PACK):
-            nc.vector.tensor_copy(notes_picked[:, t, :], note_pools[t // 2][:, t % 2, :].indirect(note_list[:]))
+            nc.vector.tensor_copy(notes_picked[:, t, :], note_pool[:, t, :].indirect(note_list[:]))
         notes_grouped = keep.tile([P, J, PACK], BF16, align_bytes=64)
         dst, src = woven(notes_grouped[:], notes_picked[:])
         nc.vector.tensor_copy(dst, src)
@@ -141,39 +154,43 @@ def tile_attend_tab_timestable_gains_pl_kernel(
 
         memories_picked = []
         for t in range(PACK):
-            looked_up = keep.tile([P, J], F32, name="memories_picked%d" % t, tag="swap%d" % (t + 1), align_bytes=64)
+            looked_up = keep.tile([P, J], F32, name="memories_picked%d" % t)
             nc.scalar.activation(looked_up[:], memories[t][:].indirect(memory_list[:]), COPY)
             memories_picked.append(looked_up)
 
-        given_picked = keep.tile([P, PACK, J], F32)
         table = keep.tile([P, PACK, J], F32)
-        for a in range(2):
-            for r in (2 * a, 2 * a + 1):
-                nc.vector.tensor_copy(given_picked[:, r, :], given_pools[a][:, r % 2, :].indirect(given_list[:]))
-            for r in (2 * a, 2 * a + 1):
-                nc.vector.scalar_tensor_tensor(
-                    table[:, r, :], products[a][:, r % 2, :], row_factor[:, r : r + 1], given_picked[:, r, :], MULT, MULT
-                )
+        for r in range(PACK):
+            given_picked = keep.tile([P, J], F32, name="given_picked%d" % r)
+            window = given_pools[r // 2][:, r % 2, :].indirect(given_list[:])
+            if r < 2:
+                nc.vector.tensor_copy(given_picked[:], window)
+            else:
+                nc.scalar.activation(given_picked[:], window, COPY)
+            nc.vector.scalar_tensor_tensor(
+                table[:, r, :], products[r // 2][:, r % 2, :], row_factor[:, r : r + 1], given_picked[:], MULT, MULT
+            )
         table_grouped = keep.tile([P, J, PACK], BF16, align_bytes=64)
         dst, src = woven(table_grouped[:], table[:])
         nc.vector.tensor_copy(dst, src)
         table_codes, table_scales = quantise(table_grouped[:].rearrange("p j r -> p (j r)"), J, "table")
 
-        result = keep.tile([P, PACK, J], F32)
         result_grouped = [keep.tile([P, HALF_J, PACK], BF16, name="result_grouped%d" % h, align_bytes=64) for h in range(2)]
-        for t in range(PACK):
-            picked = keep.tile([P, I], BF16, name="picked%d" % t, tag="memories%d" % (PACK - 1))
-            nc.scalar.activation(picked[:], value_pools[t][:].indirect(token_list[:]), COPY)
+        out_rows = out_0.rearrange("(p t) j -> p t j", t=PACK)
+        half = I // 2
+
+        def turn_values(picked):
             pairs = picked[:].bitcast(F32)
             turned = turn.tile([P, 2, P], F32)
             for u in range(2):
                 nc.tensor.transpose(turned[:, u, :], pairs[:, u : I // 2 : 2], ident[:])
-            values_grouped = keep.tile([P, P * PACK], BF16, name="values_grouped%d" % t, tag="swap%d" % t, align_bytes=64)
-            copy_out = nc.scalar.copy if t == PACK - 1 else nc.vector.tensor_copy
-            copy_out(
-                values_grouped[:].bitcast(F32).rearrange("p (e u) -> p e u", u=2), turned[:].rearrange("p u e -> p e u")
-            )
-            value_codes, value_scales = quantise(values_grouped[:], P, "values", ring)
+            return turned
+
+        def quantise_values(t, turned, copy_out, tag):
+            grouped = keep.tile([P, P * PACK], BF16, name="values_grouped%d" % t, tag=tag, align_bytes=64)
+            copy_out(grouped[:].bitcast(F32).rearrange("p (e u) -> p e u", u=2), turned[:].rearrange("p u e -> p e u"))
+            return quantise(grouped[:], P, "values%d" % t)
+
+        def multiply(t, value_codes, value_scales, result):
             sums = []
             for h in range(2):
                 cols = slice(h * HALF_J, (h + 1) * HALF_J)
@@ -185,14 +202,28 @@ def tile_attend_tab_timestable_gains_pl_kernel(
                 sums.append(bank)
             for h in range(2):
                 cols = slice(h * HALF_J, (h + 1) * HALF_J)
-                nc.vector.tensor_tensor(result[:, t, cols], sums[h][:, 0:HALF_J], memories_picked[t][:, cols], MULT)
-            for h in range(2):
-                cols = slice(h * HALF_J, (h + 1) * HALF_J)
-                nc.vector.tensor_copy(result_grouped[h][:, :, t], result[:, t, cols])
+                nc.vector.tensor_tensor(result[:, cols], sums[h][:, 0:HALF_J], memories_picked[t][:, cols], MULT)
 
-        out_rows = out_0.rearrange("(p t) j -> p t j", t=PACK)
-        nc.sync.dma_start(out_rows[:, 0 : PACK - 1, :], result[:, 0 : PACK - 1, :])
-        nc.scalar.dma_start(out_rows[:, PACK - 1, :], result[:, PACK - 1, :])
+        for first in (0, 2):
+            second = first + 1
+            picked = keep.tile([P, I], BF16, name="picked%d" % first, tag="given_pool1")
+            nc.scalar.activation(picked[:], value_pools[first][:].indirect(token_list[:]), COPY)
+            turned_first = turn_values(picked)
+            picked = keep.tile([P, I], BF16, name="picked%d" % second, tag="given_pool0")
+            nc.scalar.activation(picked[:, 0:half], value_pools[second][:].indirect(token_list[:, 0 : half // 16]), COPY)
+            nc.vector.tensor_copy(picked[:, half:I], value_pools[second][:].indirect(token_list[:, half // 16 : I // 16]))
+            turned_second = turn_values(picked)
+            first_operand = quantise_values(first, turned_first, nc.vector.tensor_copy, "value_pool%d" % second)
+            second_operand = quantise_values(second, turned_second, nc.scalar.copy, "handed_on%d" % second)
+            result = keep.tile([P, 2, J], F32, name="result%d" % first, tag="handed_on%d" % second, align_bytes=64)
+            multiply(first, *first_operand, result[:, 0, :])
+            multiply(second, *second_operand, result[:, 1, :])
+            for h in range(2):
+                dst, src = woven(result_grouped[h][:, :, first : first + 2], result[:, :, h * HALF_J : (h + 1) * HALF_J])
+                nc.vector.tensor_copy(dst, src)
+            queue = nc.sync if first == 0 else nc.scalar
+            queue.dma_start(out_rows[:, first : first + 2, :], result[:])
+
         result_codes = keep.tile([P, J], U32, align_bytes=64)
         result_scales = keep.tile([P, J], U8, align_bytes=64)
         for h in range(2):

@@ -49,7 +49,7 @@ def tile_attend_tab_timestable_gains_pl_kernel(
 
         store_rows = mstore.rearrange("(p j) m -> p j m", j=PACK)
         store_raw = [keep.tile([P, 2, M], F32, name="store_raw%d" % a) for a in range(2)]
-        nc.scalar.dma_start(store_raw[0][:], store_rows[:, 0:2, :])
+        nc.sync.dma_start(store_raw[0][:], store_rows[:, 0:2, :])
 
         key_scale_pool = keep.tile([P, T], U8, align_bytes=64)
         nc.vector.memset(key_scale_pool[:].bitcast(I32), 0)

from contextlib import ExitStack

import concourse.mybir as mybir
from concourse.masks import make_identity

D, T, I, J, U, Z, E, M, C = 512, 2048, 512, 256, 1024, 1024, 512, 1024, 512
FLOPS = 2 * D * I * J + 2 * I * E * J + 2 * C * E * M

F32 = mybir.dt.float32
BF16 = mybir.dt.bfloat16
I32 = mybir.dt.int32
U32 = mybir.dt.uint32
U16 = mybir.dt.uint16
U8 = mybir.dt.uint8
FP8X4 = mybir.dt.float8_e4m3fn_x4
FP4X4 = mybir.dt.float4_e2m1fn_x4
COPY = mybir.ActivationFunctionType.Copy
MULT = mybir.AluOpType.mult

P = 128
PACK = 4
BANK = 512
HALF_J = J // 2


def woven(dst, src):
    return (
        dst.rearrange("p (c i) t -> p c t i", i=4),
        src.rearrange("p t (c i) -> p c t i", i=4),
    )


def tile_attend_tab_timestable_gains_pl_kernel(
    tc, keys_words, keys_scales, notes, given, rowf, vals, wm, mstore, offs, offs2, offs3, offs4, out_0, out_1, out_2
):
    nc = tc.nc
    with ExitStack() as ctx:
        lists = ctx.enter_context(tc.tile_pool(name="lists", bufs=1))
        keep = ctx.enter_context(tc.tile_pool(name="keep", bufs=1))
        acc = ctx.enter_context(tc.psum_pool(name="acc", bufs=4))
        turn = ctx.enter_context(tc.psum_pool(name="turn", bufs=2))
        tab = ctx.enter_context(tc.psum_pool(name="tab", bufs=1))

        def quantise(grouped, width, name, pool=keep):
            codes = pool.tile([P, width], U32, name=name + "_codes", align_bytes=64)
            scales = pool.tile([P, width], U8, name=name + "_scales", align_bytes=64)
            nc.vector.quantize_mx(out=codes[:].bitcast(FP8X4), scales=scales[:], in_=grouped)
            return codes, scales

        store_rows = mstore.rearrange("(p j) m -> p j m", j=PACK)
        store_raw = [keep.tile([P, 2, M], F32, name="store_raw%d" % a) for a in range(2)]
        nc.sync.dma_start(store_raw[0][:], store_rows[:, 0:2, :])

        key_scale_pool = keep.tile([P, T], U8, align_bytes=64)
        nc.vector.memset(key_scale_pool[:].bitcast(I32), 0)
        nc.scalar.dma_start(key_scale_pool[0:P:8, :].bitcast(I32), keys_scales[0].bitcast(I32))
        key_scales = keep.tile([P, I], U8, align_bytes=64)
        nc.gpsimd.memset(key_scales[:].bitcast(I32), 0)
        row_factor = keep.tile([P, PACK], F32)
        nc.scalar.dma_start(row_factor[:], rowf.rearrange("(p r) o -> p (r o)", r=PACK))
        ident = keep.tile([P, P], F32)
        make_identity(nc, ident[:])

        token_list = lists.tile([P, I // 16], U16)
        nc.sync.dma_start(token_list[:], offs)
        note_list = lists.tile([P, J // 16], U16)
        nc.sync.dma_start(note_list[:], offs2)
        given_list = lists.tile([P, J // 16], U16)
        nc.sync.dma_start(given_list[:], offs3)
        memory_list = lists.tile([P, J // 16], U16)
        nc.sync.dma_start(memory_list[:], offs4)
        wm_raw = keep.tile([P, PACK, E], F32)
        nc.sync.dma_start(wm_raw[:], wm.rearrange("(p j) e -> p j e", j=PACK))
        nc.sync.dma_start(store_raw[1][:], store_rows[:, 2:4, :])
        key_word_pool = keep.tile([P, T], U16, align_bytes=64)
        nc.sync.dma_start(key_word_pool[:].bitcast(I32), keys_words[0].bitcast(I32))
        note_pool = keep.tile([P, PACK, U], F32)
        nc.sync.dma_start(note_pool[:], notes.rearrange("(p t) u -> p t u", t=PACK))
        given_rows = given.rearrange("(p r) z -> p r z", r=PACK)
        given_pools = []
        for a in range(2):
            pool_tile = keep.tile([P, 2, Z], F32, name="given_pool%d" % a, tag="given_pool%d" % a)
            nc.sync.dma_start(pool_tile[:], given_rows[:, 2 * a : 2 * a + 2, :])
            given_pools.append(pool_tile)
        vals_rows = vals.rearrange("(p t) n -> p t n", t=PACK)
        value_pools = []
        for t in range(PACK):
            pool_tile = keep.tile([P, T], F32, name="value_pool%d" % t, tag="value_pool%d" % t, align_bytes=64)
            nc.sync.dma_start(pool_tile[:], vals_rows[:, t, :])
            value_pools.append(pool_tile)

        store_grouped = [
            keep.tile([P, BANK, PACK], BF16, name="store_grouped%d" % h, tag="store_grouped%d" % h, align_bytes=64)
            for h in range(2)
        ]

        def round_store(a, h):
            dst, src = woven(store_grouped[h][:, :, 2 * a : 2 * a + 2], store_raw[a][:, :, h * BANK : (h + 1) * BANK])
            if a == 0:
                nc.scalar.activation(dst, src, COPY)
            else:
                nc.vector.tensor_copy(dst, src)

        round_store(0, 0)
        round_store(0, 1)
        wm_grouped = keep.tile([P, E * PACK], BF16, align_bytes=64)
        nc.vector.tensor_copy(
            wm_grouped[:].rearrange("p (t s j) -> p s j t", t=PACK, j=PACK),
            wm_raw[:].rearrange("p j (s t) -> p s j t", t=PACK),
        )
        wm_codes, wm_scales = quantise(wm_grouped[:], E, "wm")
        scales_picked = keep.tile([P, I], U8, align_bytes=64)
        nc.vector.tensor_copy(
            scales_picked[:].rearrange("p (r s) -> p s r", r=PACK), key_scale_pool[:].indirect(token_list[:])
        )
        for q in range(4):
            nc.scalar.dma_start(
                key_scales[32 * q : 32 * q + 4, :].bitcast(I32), scales_picked[32 * q : 32 * q + 32 : 8, :].bitcast(I32)
            )

        memories = [keep.tile([P, M], F32, name="memories%d" % t, tag="memories%d" % t) for t in range(PACK)]
        round_store(1, 0)
        round_store(1, 1)
        for h in range(2):
            codes, scales = quantise(store_grouped[h][:].rearrange("p m j -> p (m j)"), BANK, "store%d" % h)
            for t in range(PACK):
                bank = acc.tile([P, BANK], F32, name="bank")
                cols = slice(t * P, (t + 1) * P)
                nc.tensor.matmul_mx(
                    out=bank[:], lhsT=wm_codes[:, cols].bitcast(FP8X4), lhsT_scale=wm_scales[:, cols],
                    rhs=codes[:].bitcast(FP8X4), rhs_scale=scales[:], start=True, stop=True,
                )
                nc.scalar.activation(memories[t][:, h * BANK : (h + 1) * BANK], bank[:], COPY)

        key_words = keep.tile([P, I], U16, tag="store_grouped0", align_bytes=64)
        nc.vector.tensor_copy(key_words[:], key_word_pool[:].indirect(token_list[:]))
        key_dealt = keep.tile([P, PACK, P], U16, align_bytes=64)
        nc.vector.tensor_copy(key_dealt[:], key_words[:].rearrange("p (s r) -> p r s", r=PACK))

        notes_picked = keep.tile([P, PACK, J], F32)
        for t in range(PACK):
            nc.vector.tensor_copy(notes_picked[:, t, :], note_pool[:, t, :].indirect(note_list[:]))
        notes_grouped = keep.tile([P, J, PACK], BF16, align_bytes=64)
        dst, src = woven(notes_grouped[:], notes_picked[:])
        nc.vector.tensor_copy(dst, src)
        note_codes, note_scales = quantise(notes_grouped[:].rearrange("p j t -> p (j t)"), J, "notes")
        products = [tab.tile([P, 2, J], F32, name="products%d" % a) for a in range(2)]
        for r in range(PACK):
            nc.tensor.matmul_mx(
                out=products[r // 2][:, r % 2, :], lhsT=key_dealt[:, r, :].bitcast(FP4X4),
                lhsT_scale=key_scales[:, r * P : (r + 1) * P],
                rhs=note_codes[:].bitcast(FP8X4), rhs_scale=note_scales[:], start=True, stop=True,
            )

        memories_picked = []
        for t in range(PACK):
            looked_up = keep.tile([P, J], F32, name="memories_picked%d" % t)
            nc.scalar.activation(looked_up[:], memories[t][:].indirect(memory_list[:]), COPY)
            memories_picked.append(looked_up)

        table = keep.tile([P, PACK, J], F32)
        for r in range(PACK):
            given_picked = keep.tile([P, J], F32, name="given_picked%d" % r)
            window = given_pools[r // 2][:, r % 2, :].indirect(given_list[:])
            if r < 2:
                nc.vector.tensor_copy(given_picked[:], window)
            else:
                nc.scalar.activation(given_picked[:], window, COPY)
            nc.vector.scalar_tensor_tensor(
                table[:, r, :], products[r // 2][:, r % 2, :], row_factor[:, r : r + 1], given_picked[:], MULT, MULT
            )
        table_grouped = keep.tile([P, J, PACK], BF16, align_bytes=64)
        dst, src = woven(table_grouped[:], table[:])
        nc.vector.tensor_copy(dst, src)
        table_codes, table_scales = quantise(table_grouped[:].rearrange("p j r -> p (j r)"), J, "table")

        result_grouped = [keep.tile([P, HALF_J, PACK], BF16, name="result_grouped%d" % h, align_bytes=64) for h in range(2)]
        out_rows = out_0.rearrange("(p t) j -> p t j", t=PACK)
        half = I // 2

        def turn_values(picked):
            pairs = picked[:].bitcast(F32)
            turned = turn.tile([P, 2, P], F32)
            for u in range(2):
                nc.tensor.transpose(turned[:, u, :], pairs[:, u : I // 2 : 2], ident[:])
            return turned

        def quantise_values(t, turned, copy_out, tag):
            grouped = keep.tile([P, P * PACK], BF16, name="values_grouped%d" % t, tag=tag, align_bytes=64)
            copy_out(grouped[:].bitcast(F32).rearrange("p (e u) -> p e u", u=2), turned[:].rearrange("p u e -> p e u"))
            return quantise(grouped[:], P, "values%d" % t)

        def multiply(t, value_codes, value_scales, result):
            sums = []
            for h in range(2):
                cols = slice(h * HALF_J, (h + 1) * HALF_J)
                bank = acc.tile([P, BANK], F32, name="bank")
                nc.tensor.matmul_mx(
                    out=bank[:, 0:HALF_J], lhsT=value_codes[:].bitcast(FP8X4), lhsT_scale=value_scales[:],
                    rhs=table_codes[:, cols].bitcast(FP8X4), rhs_scale=table_scales[:, cols], start=True, stop=True,
                )
                sums.append(bank)
            for h in range(2):
                cols = slice(h * HALF_J, (h + 1) * HALF_J)
                nc.vector.tensor_tensor(result[:, cols], sums[h][:, 0:HALF_J], memories_picked[t][:, cols], MULT)

        for first in (0, 2):
            second = first + 1
            picked = keep.tile([P, I], BF16, name="picked%d" % first, tag="given_pool1")
            nc.scalar.activation(picked[:], value_pools[first][:].indirect(token_list[:]), COPY)
            turned_first = turn_values(picked)
            picked = keep.tile([P, I], BF16, name="picked%d" % second, tag="given_pool0")
            nc.scalar.activation(picked[:, 0:half], value_pools[second][:].indirect(token_list[:, 0 : half // 16]), COPY)
            nc.vector.tensor_copy(picked[:, half:I], value_pools[second][:].indirect(token_list[:, half // 16 : I // 16]))
            turned_second = turn_values(picked)
            first_operand = quantise_values(first, turned_first, nc.vector.tensor_copy, "value_pool%d" % second)
            second_operand = quantise_values(second, turned_second, nc.scalar.copy, "handed_on%d" % second)
            result = keep.tile([P, 2, J], F32, name="result%d" % first, tag="handed_on%d" % second, align_bytes=64)
            multiply(first, *first_operand, result[:, 0, :])
            multiply(second, *second_operand, result[:, 1, :])
            for h in range(2):
                dst, src = woven(result_grouped[h][:, :, first : first + 2], result[:, :, h * HALF_J : (h + 1) * HALF_J])
                nc.vector.tensor_copy(dst, src)
            queue = nc.sync if first == 0 else nc.scalar
            queue.dma_start(out_rows[:, first : first + 2, :], result[:])

        result_codes = keep.tile([P, J], U32, align_bytes=64)
        result_scales = keep.tile([P, J], U8, align_bytes=64)
        for h in range(2):
            cols = slice(h * HALF_J, (h + 1) * HALF_J)
            nc.vector.quantize_mx(
                out=result_codes[:, cols].bitcast(FP8X4), scales=result_scales[:, cols],
                in_=result_grouped[h][:].rearrange("p j t -> p (j t)"),
            )
        nc.sync.dma_start(out_1[0].rearrange("p c r -> p (c r)").bitcast(I32), result_codes[:].bitcast(I32))
        for q in range(4):
            queue = nc.sync if q < 2 else nc.scalar
            queue.dma_start(
                out_2[0, 4 * q : 4 * q + 4, :].bitcast(I32), result_scales[32 * q : 32 * q + 4, :].bitcast(I32)
            )
